import numpy as np
import ml_dtypes


def mxq(x, axis, fmt="e4m3"):
    dtype, down = {"e4m3": (ml_dtypes.float8_e4m3fn, 7), "e5m2": (ml_dtypes.float8_e5m2, 14)}[fmt]
    v = np.moveaxis(np.asarray(x, np.float32).astype(ml_dtypes.bfloat16).astype(np.float64), axis, -1)
    blocks = v.reshape(v.shape[:-1] + (-1, 32))
    amax = np.abs(blocks).max(-1, keepdims=True)
    byte = np.maximum(np.where(amax > 0, np.frexp(amax)[1] - 1 + 127, 0) - down, 1)
    scale = np.exp2(byte - 127.0)
    codes = (blocks / scale).astype(np.float32).astype(dtype).astype(np.float64)
    return np.moveaxis((codes * scale).reshape(v.shape), -1, axis)


WIDE = False


def mx_kscale(k):
    if not WIDE:
        return np.ones(k)
    levels = np.array([10, -10, 5, -5, 0])
    if k % 512:
        return np.exp2(np.random.permutation(np.resize(levels, k // 32))).repeat(32)
    a = np.empty((k // 512, 16))
    for p in range(k // 512):
        a[p, :8] = np.random.permutation(np.resize(levels, 8))
        for g in range(8):
            far = levels[np.abs(levels - a[p, g]) >= 10]
            a[p, g + 8] = far[np.random.randint(len(far))]
    return np.exp2(a.ravel()).repeat(32)


def f64(x):
    return np.asarray(x).astype(np.float64)


def striped(idx):
    return np.tile(np.asarray(idx).reshape(-1, 16).T, (8, 1)).astype(np.uint16)


def unstriped(offs):
    return offs[:16].T.reshape(-1).astype(np.int64)


E2M1 = np.array([0.0, 0.5, 1.0, 1.5, 2.0, 3.0, 4.0, 6.0, -0.0, -0.5, -1.0, -1.5, -2.0, -3.0, -4.0, -6.0])


def pack_weight(w, fmt):
    k, n = w.shape
    w = f64(np.asarray(w, np.float32).astype(ml_dtypes.bfloat16)).reshape(k // 32, 32, n)
    amax = np.abs(w).max(1)
    if fmt == "e4m3":
        byte = np.frexp(amax)[1] - 1 + 127 - 7
    else:
        mant, ex = np.frexp(amax / 6.0)
        byte = np.where(mant > 0.5, ex, ex - 1) + 127
    byte = np.clip(np.where(amax > 0, byte, 1), 1, 254)
    scaled = (w * np.exp2(127.0 - byte)[:, None, :]).reshape(k, n).astype(np.float32)
    by_word = np.ascontiguousarray(scaled.reshape(k // 512, 128, 4, n).transpose(0, 1, 3, 2))
    if fmt == "e4m3":
        words = by_word.astype(ml_dtypes.float8_e4m3fn).view(np.uint8)
    else:
        c = by_word.astype(ml_dtypes.float4_e2m1fn).view(np.uint8) & 0xF
        words = (c[..., 0::2] | (c[..., 1::2] << 4)).reshape(k // 512, 128, 2 * n)
    return np.ascontiguousarray(words), np.ascontiguousarray(byte.astype(np.uint8).reshape(k // 512, 16, n))


def unpack_weight(words, scales, fmt):
    g, _, n = scales.shape
    words = np.ascontiguousarray(words).reshape(g, 128, n, -1)
    if fmt == "e4m3":
        vals = words.view(ml_dtypes.float8_e4m3fn).astype(np.float64)
    else:
        nib = np.empty((g, 128, n, 4), np.uint8)
        nib[..., 0::2] = words & 0xF
        nib[..., 1::2] = words >> 4
        vals = E2M1[nib]
    vals = vals * np.repeat(np.exp2(scales.astype(np.float64) - 127.0), 8, axis=1)[..., None]
    return vals.transpose(0, 1, 3, 2).reshape(g * 512, n)


D, T, I, Q, U = 512, 1024, 256, 512, 1024


def setup_inputs():
    n = np.random.standard_normal
    idx = np.random.permutation(T)[:I]
    idx4 = np.random.permutation(U)[:Q]
    fd = mx_kscale(D)
    fq = mx_kscale(Q)
    qpoolp = pack_weight(n((D, U)) * 0.03 * fd[:, None], "e4m3")
    return {
        "keys": (n((D, T))).astype(np.float32),
        "qpool_words": qpoolp[0],
        "qpool_scales": qpoolp[1],
        "ksc": (np.random.uniform(0.5, 2.0, (D, 1)) / fd[:, None]).astype(np.float32),
        "qs": (np.random.uniform(16.0, 64.0, (Q, 1)) * fq[:, None]).astype(np.float32),
        "target": (np.random.uniform(0.0, 0.008, (Q, I))).astype(np.float32),
        "qrows": (n((Q, D)) / fq[:, None]).astype(np.float32),
        "softn": (np.random.uniform(0.3, 1.5, (D, 1))).astype(np.float32),
        "pre": (np.random.uniform(0.6, 1.6, (1, I))).astype(np.float32),
        "sg": (np.random.uniform(0.5, 2.0, (1, I))).astype(np.float32),
        "old": (n((D, T)) * 1.0).astype(np.float32),
        "fade": (np.random.uniform(0.5, 1.0, (1, T))).astype(np.float32),
        "offs": striped(idx),
        "offs4": striped(idx4),
    }


def reference(keys, qpool_words, qpool_scales, ksc, qs, target, qrows, softn, pre, sg, old, fade, offs, offs4):
    idx = unstriped(offs)
    idx4 = unstriped(offs4)
    qpoolu = unpack_weight(qpool_words, qpool_scales, "e4m3")
    x1 = f64(keys)[:, idx] * f64(pre)
    vp = x1 / (np.square(x1) * f64(softn) + 1.0)
    kp = vp * f64(ksc)
    qpoolidx4g = qpoolu[:, idx4]
    kpq = mxq(kp, 0, "e4m3")
    a = qpoolidx4g.T @ kpq
    p = np.exp(a - np.max(a, axis=1, keepdims=True))
    ds = (p / np.sum(p, axis=1, keepdims=True) - f64(target)) * f64(qs)
    qrowsq = mxq(f64(qrows), 0, "e4m3")
    dsq = mxq(ds, 0, "e4m3")
    c0 = qrowsq.T @ dsq
    dx1 = c0 / (np.square(x1) * f64(softn) + 1.0) + c0 * x1 / np.square(np.square(x1) * f64(softn) + 1.0) * (-1.0) * f64(softn) * x1 * 2.0
    gs = dx1 * f64(sg)
    gf = np.zeros((D, T))
    gf[:, idx] = gs
    y = f64(old) * f64(fade) + gf
    return y

import math
from contextlib import ExitStack

import concourse.mybir as mybir
from concourse.masks import make_identity

D, T, I, Q, U = 512, 1024, 256, 512, 1024
FLOPS = 2 * 2 * D * Q * I

F32 = mybir.dt.float32
BF16 = mybir.dt.bfloat16
I32 = mybir.dt.int32
U32 = mybir.dt.uint32
U16 = mybir.dt.uint16
U8 = mybir.dt.uint8
FP8X4 = mybir.dt.float8_e4m3fn_x4
ALU = mybir.AluOpType
ACT = mybir.ActivationFunctionType
AXIS_X = mybir.AxisListType.X

P = 128
PACK = 4
BANK = 512
HALVES = T // BANK
CHUNKS = BANK // P


def tile_attend_bksoftened_s_kernel(tc, keys, qpool_words, qpool_scales, ksc, qs, target, qrows, softn, pre, sg, old, fade, offs, offs4, out):
    nc = tc.nc
    with ExitStack() as ctx:
        lists = ctx.enter_context(tc.tile_pool(name="lists", bufs=1))
        sb = ctx.enter_context(tc.tile_pool(name="sb", bufs=1))
        ps = ctx.enter_context(tc.psum_pool(name="ps", bufs=1))

        def bank(tag, bufs):
            return ps.tile([P, BANK], F32, name=tag, tag=tag, bufs=bufs)

        slot_list = lists.tile([P, I // 16], U16, name="slot_list")
        query_list = lists.tile([P, Q // 16], U16, name="query_list")
        pre_col = sb.tile([P, I // P], F32, name="pre_col")
        sg_col = sb.tile([P, I // P], F32, name="sg_col")
        softn_col = sb.tile([P, PACK], F32, name="softn_col")
        ksc_col = sb.tile([P, PACK], F32, name="ksc_col")
        qs_col = sb.tile([P, PACK], F32, name="qs_col")
        key_planes = [sb.tile([P, T], F32, name="keys%d" % j) for j in range(PACK)]
        pool_words = sb.tile([P, U], U32, name="pool_words")
        pool_scales = sb.tile([P, U], U8, name="pool_scales")
        qrows_raw = sb.tile([P, PACK, D], F32, name="qrows_raw")
        target_raw = sb.tile([P, PACK, I], F32, name="target_raw")
        old_halves = [sb.tile([P, PACK, BANK], F32, name="old%d" % h) for h in range(HALVES)]
        fade_rows = sb.tile([P, P], F32, name="fade_rows")
        windows = [sb.tile([P, T], F32, name="window%d" % j) for j in range(PACK)]
        ident = sb.tile([P, P], F32, name="ident")

        nc.gpsimd.memset(pool_scales[:].bitcast(I32), 0)
        nc.vector.memset(fade_rows[:], 0.0)
        make_identity(nc, ident[:])
        for j in range(PACK // 2):
            nc.vector.memset(windows[j][:], 0.0)

        keys_by_plane = keys.rearrange("(p j) t -> p j t", j=PACK)
        old_by_plane = old.rearrange("(p j) t -> p j t", j=PACK)
        out_by_plane = out.rearrange("(p j) t -> p j t", j=PACK)

        nc.sync.dma_start(slot_list[:], offs)
        nc.sync.dma_start(pre_col[:], pre.rearrange("o (p c) -> (o p) c", p=P))
        nc.sync.dma_start(softn_col[:], softn.rearrange("(p j) o -> p (j o)", j=PACK))
        for j in range(PACK):
            nc.sync.dma_start(key_planes[j][:], keys_by_plane[:, j, :])
        nc.sync.dma_start(query_list[:], offs4)
        nc.sync.dma_start(pool_words[:].bitcast(I32), qpool_words[0].rearrange("p n t -> p (n t)").bitcast(I32))
        nc.sync.dma_start(ksc_col[:], ksc.rearrange("(p j) o -> p (j o)", j=PACK))
        nc.sync.dma_start(qs_col[:], qs.rearrange("(p j) o -> p (j o)", j=PACK))
        nc.sync.dma_start(target_raw[:], target.rearrange("(p j) i -> p j i", j=PACK))
        nc.sync.dma_start(qrows_raw[:], qrows.rearrange("(p j) d -> p j d", j=PACK))
        nc.sync.dma_start(sg_col[:], sg.rearrange("o (p c) -> (o p) c", p=P))
        for h in range(HALVES):
            nc.sync.dma_start(old_halves[h][:], old_by_plane[:, :, h * BANK : (h + 1) * BANK])

        for quad in range(4):
            nc.gpsimd.dma_start(
                pool_scales[32 * quad : 32 * quad + 4, :].bitcast(I32),
                qpool_scales[0, 4 * quad : 4 * quad + 4, :].bitcast(I32),
            )
        nc.gpsimd.dma_start(fade_rows[0 : T // P, :], fade.rearrange("o (c m) -> (o c) m", m=P))
        for j in range(PACK // 2, PACK):
            nc.gpsimd.memset(windows[j][:], 0.0)

        def spread_over_partitions(col, name, copy):
            turned = bank("stage", 2)
            n = col.shape[1]
            for c in range(n):
                nc.tensor.transpose(turned[:, c * P : (c + 1) * P], col[:, c : c + 1].to_broadcast([P, P]), ident[:])
            row = sb.tile([P, P, n], F32, name=name)
            copy(row[:], turned[:, 0 : n * P].rearrange("p (c m) -> p m c", c=n))
            return row[:].rearrange("p m c -> p (m c)")

        pre_row = spread_over_partitions(pre_col, "pre_row", nc.vector.tensor_copy)

        x1 = sb.tile([P, PACK, I], F32, name="x1")
        x1_sq = sb.tile([P, PACK, I], F32, name="x1_sq", tag="square_then_inverse")
        log_den = sb.tile([P, PACK, I], F32, name="log_den", tag="log_then_qrows", align_bytes=64)
        kp_planes = sb.tile([P, PACK, I], BF16, name="kp_planes")
        for j in range(PACK):
            nc.vector.tensor_tensor(x1[:, j, :], key_planes[j][:].indirect(slot_list[:]), pre_row, ALU.mult)
            if j == 0:
                nc.vector.tensor_tensor(x1_sq[:, j, :], x1[:, j, :], x1[:, j, :], ALU.mult)
            else:
                nc.scalar.activation(x1_sq[:, j, :], x1[:, j, :], ACT.Square)
            nc.scalar.activation(log_den[:, j, :], x1_sq[:, j, :], ACT.Ln, scale=softn_col[:, j : j + 1], bias=1.0)
        inv_den = sb.tile([P, PACK, I], F32, name="inv_den", tag="square_then_inverse")
        for j in range(PACK):
            nc.scalar.activation(inv_den[:, j, :], log_den[:, j, :], ACT.Exp, scale=-1.0)
            nc.vector.scalar_tensor_tensor(kp_planes[:, j, :], x1[:, j, :], ksc_col[:, j : j + 1], inv_den[:, j, :], ALU.mult, ALU.mult)

        def interleave(dst, src):
            nc.vector.tensor_copy(
                dst[:].rearrange("p (c i) t -> p c t i", i=4),
                src[:].rearrange("p t (c i) -> p c t i", i=4),
            )

        def quantise(src, width, name):
            words = sb.tile([P, width], U32, name=name + "_words", align_bytes=64)
            scales = sb.tile([P, width], U8, name=name + "_scales", align_bytes=64)
            nc.vector.quantize_mx(out=words[:].bitcast(FP8X4), scales=scales[:], in_=src)
            return words, scales

        kp_woven = sb.tile([P, I, PACK], BF16, name="kp_woven", align_bytes=64)
        interleave(kp_woven, kp_planes)

        query_words = sb.tile([P, Q], U32, name="query_words", align_bytes=64)
        listed_scales = sb.tile([P, Q], U8, name="listed_scales")
        query_scales = sb.tile([P, Q], U8, name="query_scales", align_bytes=64)
        nc.vector.tensor_copy(listed_scales[:], pool_scales[:].indirect(query_list[:]))
        nc.vector.tensor_copy(query_words[:].rearrange("p (r s) -> p s r", r=PACK), pool_words[:].indirect(query_list[:]))
        nc.vector.tensor_copy(
            query_scales[:].rearrange("p (r s) -> p r s", r=PACK),
            listed_scales[:].rearrange("p (s r) -> p r s", r=PACK),
        )
        kp_words, kp_scales = quantise(kp_woven[:].rearrange("p i t -> p (i t)"), I, "kp")

        def product(stat_words, stat_scales, mov_words, mov_scales):
            banks = []
            for r in range(PACK):
                b = bank("sums", 6)
                cols = slice(r * P, (r + 1) * P)
                nc.tensor.matmul_mx(
                    out=b[:, 0:I],
                    lhsT=stat_words[:, cols].bitcast(FP8X4),
                    lhsT_scale=stat_scales[:, cols],
                    rhs=mov_words[:].bitcast(FP8X4),
                    rhs_scale=mov_scales[:],
                    start=True,
                    stop=True,
                )
                banks.append(b)
            return banks

        score_banks = product(query_words, query_scales, kp_words, kp_scales)

        scaled_target = sb.tile([P, PACK, I], F32, name="scaled_target")
        for r in range(PACK):
            nc.vector.tensor_scalar(scaled_target[:, r, :], target_raw[:, r, :], qs_col[:, r : r + 1], None, ALU.mult)

        probs = sb.tile([P, PACK, I], F32, name="probs")
        ds_planes = sb.tile([P, PACK, I], BF16, name="ds_planes")
        neg_max = [sb.tile([P, 1], F32, name="neg_max%d" % r) for r in range(PACK)]
        row_sum = [sb.tile([P, 1], F32, name="row_sum%d" % r) for r in range(PACK)]
        inv_sum = [sb.tile([P, 1], F32, name="inv_sum%d" % r) for r in range(PACK)]
        row_gain = [sb.tile([P, 1], F32, name="row_gain%d" % r) for r in range(PACK)]
        for r in range(PACK):
            scores = score_banks[r][:, 0:I]
            nc.vector.tensor_reduce(neg_max[r][:], scores, AXIS_X, ALU.max, negate=True)
            nc.scalar.activation(probs[:, r, :], scores, ACT.Exp, bias=neg_max[r][:], accum_out=row_sum[r][:])
        for r in range(PACK):
            nc.vector.reciprocal(inv_sum[r][:], row_sum[r][:])
            nc.vector.tensor_tensor(row_gain[r][:], inv_sum[r][:], qs_col[:, r : r + 1], ALU.mult)
            nc.vector.scalar_tensor_tensor(ds_planes[:, r, :], probs[:, r, :], row_gain[r][:], scaled_target[:, r, :], ALU.mult, ALU.subtract)
        ds_woven = sb.tile([P, I, PACK], BF16, name="ds_woven", align_bytes=64)
        interleave(ds_woven, ds_planes)

        qrows_woven = sb.tile([P, PACK, P, PACK], BF16, name="qrows_woven", tag="log_then_qrows", align_bytes=64)
        qrows_src = qrows_raw[:].rearrange("p j (m t) -> p m t j", t=PACK)
        qrows_dst = qrows_woven[:].rearrange("p t m j -> p m t j")
        piece = P // 4
        for k in range(4):
            nc.scalar.copy(qrows_dst[:, k * piece : (k + 1) * piece], qrows_src[:, k * piece : (k + 1) * piece])
        qrows_words, qrows_scales = quantise(qrows_woven[:].rearrange("p t m j -> p (t m j)"), D, "qrows")
        ds_words, ds_scales = quantise(ds_woven[:].rearrange("p i r -> p (i r)"), I, "ds")

        grad_banks = product(qrows_words, qrows_scales, ds_words, ds_scales)

        sg_row = spread_over_partitions(sg_col, "sg_row", nc.scalar.copy)
        shifted_sq = sb.tile([P, PACK, I], F32, name="shifted_sq")
        chain = sb.tile([P, PACK, I], F32, name="chain")
        for j in range(PACK):
            nc.scalar.activation(shifted_sq[:, j, :], inv_den[:, j, :], ACT.Square, scale=math.sqrt(2.0), bias=-math.sqrt(2.0) / 4)
            nc.vector.scalar_tensor_tensor(chain[:, j, :], shifted_sq[:, j, :], 0.125, sg_row, ALU.subtract, ALU.mult)

        c0 = sb.tile([P, PACK, I], F32, name="c0")
        for j in range(PACK):
            nc.scalar.copy(c0[:, j, :], grad_banks[j][:, 0:I])
            nc.vector.tensor_tensor(windows[j][:].indirect(slot_list[:]), c0[:, j, :], chain[:, j, :], ALU.mult)

        turned_fade = bank("stage", 2)
        nc.tensor.transpose(turned_fade[:, 0:P], fade_rows[:], ident[:])
        fade_col = sb.tile([P, T // P], F32, name="fade_col")
        nc.scalar.copy(fade_col[:], turned_fade[:, 0 : T // P])

        faded_t = [sb.tile([P, D], F32, name="faded_t%d" % c) for c in range(T // P)]
        for c in range(T // P):
            h, cc = divmod(c, CHUNKS)
            turned = bank("stage", 2)
            for j in range(PACK):
                nc.tensor.transpose(turned[:, j * P : (j + 1) * P], old_halves[h][:, j, cc * P : (cc + 1) * P], ident[:])
            nc.scalar.activation(faded_t[c][:], turned[:], ACT.Copy, scale=fade_col[:, c : c + 1])

        for j in range(PACK):
            for h in range(HALVES):
                faded = bank("sums", 6)
                for cc in range(CHUNKS):
                    nc.tensor.transpose(faded[:, cc * P : (cc + 1) * P], faded_t[h * CHUNKS + cc][:, j * P : (j + 1) * P], ident[:])
                result = sb.tile([P, BANK], F32, name="result%d_%d" % (j, h))
                nc.vector.tensor_tensor(result[:], faded[:], windows[j][:, h * BANK : (h + 1) * BANK], ALU.add)
                nc.sync.dma_start(out_by_plane[:, j, h * BANK : (h + 1) * BANK], result[:])
